import numpy as np
import ml_dtypes


def mxq(x, axis, fmt="e4m3"):
    dtype, down = {"e4m3": (ml_dtypes.float8_e4m3fn, 7), "e5m2": (ml_dtypes.float8_e5m2, 14)}[fmt]
    v = np.moveaxis(np.asarray(x, np.float32).astype(ml_dtypes.bfloat16).astype(np.float64), axis, -1)
    blocks = v.reshape(v.shape[:-1] + (-1, 32))
    amax = np.abs(blocks).max(-1, keepdims=True)
    byte = np.maximum(np.where(amax > 0, np.frexp(amax)[1] - 1 + 127, 0) - down, 1)
    scale = np.exp2(byte - 127.0)
    codes = (blocks / scale).astype(np.float32).astype(dtype).astype(np.float64)
    return np.moveaxis((codes * scale).reshape(v.shape), -1, axis)


WIDE = False


def mx_kscale(k):
    if not WIDE:
        return np.ones(k)
    levels = np.array([10, -10, 5, -5, 0])
    if k % 512:
        return np.exp2(np.random.permutation(np.resize(levels, k // 32))).repeat(32)
    a = np.empty((k // 512, 16))
    for p in range(k // 512):
        a[p, :8] = np.random.permutation(np.resize(levels, 8))
        for g in range(8):
            far = levels[np.abs(levels - a[p, g]) >= 10]
            a[p, g + 8] = far[np.random.randint(len(far))]
    return np.exp2(a.ravel()).repeat(32)


def f64(x):
    return np.asarray(x).astype(np.float64)


def striped(idx):
    return np.tile(np.asarray(idx).reshape(-1, 16).T, (8, 1)).astype(np.uint16)


def unstriped(offs):
    return offs[:16].T.reshape(-1).astype(np.int64)


E2M1 = np.array([0.0, 0.5, 1.0, 1.5, 2.0, 3.0, 4.0, 6.0, -0.0, -0.5, -1.0, -1.5, -2.0, -3.0, -4.0, -6.0])


def pack_weight(w, fmt):
    k, n = w.shape
    w = f64(np.asarray(w, np.float32).astype(ml_dtypes.bfloat16)).reshape(k // 32, 32, n)
    amax = np.abs(w).max(1)
    if fmt == "e4m3":
        byte = np.frexp(amax)[1] - 1 + 127 - 7
    else:
        mant, ex = np.frexp(amax / 6.0)
        byte = np.where(mant > 0.5, ex, ex - 1) + 127
    byte = np.clip(np.where(amax > 0, byte, 1), 1, 254)
    scaled = (w * np.exp2(127.0 - byte)[:, None, :]).reshape(k, n).astype(np.float32)
    by_word = np.ascontiguousarray(scaled.reshape(k // 512, 128, 4, n).transpose(0, 1, 3, 2))
    if fmt == "e4m3":
        words = by_word.astype(ml_dtypes.float8_e4m3fn).view(np.uint8)
    else:
        c = by_word.astype(ml_dtypes.float4_e2m1fn).view(np.uint8) & 0xF
        words = (c[..., 0::2] | (c[..., 1::2] << 4)).reshape(k // 512, 128, 2 * n)
    return np.ascontiguousarray(words), np.ascontiguousarray(byte.astype(np.uint8).reshape(k // 512, 16, n))


def unpack_weight(words, scales, fmt):
    g, _, n = scales.shape
    words = np.ascontiguousarray(words).reshape(g, 128, n, -1)
    if fmt == "e4m3":
        vals = words.view(ml_dtypes.float8_e4m3fn).astype(np.float64)
    else:
        nib = np.empty((g, 128, n, 4), np.uint8)
        nib[..., 0::2] = words & 0xF
        nib[..., 1::2] = words >> 4
        vals = E2M1[nib]
    vals = vals * np.repeat(np.exp2(scales.astype(np.float64) - 127.0), 8, axis=1)[..., None]
    return vals.transpose(0, 1, 3, 2).reshape(g * 512, n)


def sigmoid(v):
    return 1.0 / (1.0 + np.exp(-v))


K, T, J, L, N = 512, 2048, 512, 512, 512


def setup_inputs():
    n = np.random.standard_normal
    idx = np.random.permutation(T)[:J]
    fk = mx_kscale(K)
    fl = mx_kscale(L)
    wp = pack_weight(n((K, N)) * 1 / np.sqrt(K) * fk[:, None], "e2m1")
    pxp = pack_weight(n((L, J)) / fl[:, None], "e4m3")
    wpp = pack_weight(n((L, N)) * 1 / np.sqrt(L) * fl[:, None], "e2m1")
    return {
        "xf": (n((K, T)) / fk[:, None]).astype(np.float32),
        "w_words": wp[0],
        "w_scales": wp[1],
        "px_words": pxp[0],
        "px_scales": pxp[1],
        "wp_words": wpp[0],
        "wp_scales": wpp[1],
        "offs": striped(idx),
    }


def reference(xf, w_words, w_scales, px_words, px_scales, wp_words, wp_scales, offs):
    idx = unstriped(offs)
    wu = unpack_weight(w_words, w_scales, "e2m1")
    pxu = unpack_weight(px_words, px_scales, "e4m3")
    wpu = unpack_weight(wp_words, wp_scales, "e2m1")
    xg = f64(xf)[:, idx]
    xp = np.pad(xg, ((0, 0), (1, 0)))[:, :J]
    d = xg - xp
    dq = mxq(d, 0, "e4m3")
    p = wu.T @ dq
    q = wpu.T @ pxu
    y = p * sigmoid(q)
    return y

@@ -1,0 +1,118 @@
+from contextlib import ExitStack
+
+import concourse.mybir as mybir
+
+K, T, J, N = 512, 2048, 512, 512
+FLOPS = 2 * 2 * K * N * J
+
+F32 = mybir.dt.float32
+BF16 = mybir.dt.bfloat16
+I32 = mybir.dt.int32
+U32 = mybir.dt.uint32
+U16 = mybir.dt.uint16
+U8 = mybir.dt.uint8
+FP8X4 = mybir.dt.float8_e4m3fn_x4
+FP4X4 = mybir.dt.float4_e2m1fn_x4
+SUB = mybir.AluOpType.subtract
+MULT = mybir.AluOpType.mult
+SIGMOID = mybir.ActivationFunctionType.Sigmoid
+
+P = 128
+PACK = 4
+HALF = J // 2
+LEAD = 8
+
+
+def tile_list_steps_along_track_kernel(tc, xf, w_words, w_scales, px_words, px_scales, wp_words, wp_scales, offs, out):
+    nc = tc.nc
+    with ExitStack() as ctx:
+        keep = ctx.enter_context(tc.tile_pool(name="keep", bufs=1))
+        psum = ctx.enter_context(tc.psum_pool(name="psum", bufs=1))
+
+        offsets = keep.tile([P, J // 16], U16, name="offsets")
+        planes = [keep.tile([P, T], F32, name="plane%d" % t) for t in range(PACK)]
+        picked = [keep.tile([P, LEAD + J], F32, name="picked%d" % t) for t in range(PACK)]
+        steps = keep.tile([P, PACK, J], BF16, name="steps")
+        woven = [keep.tile([P, HALF, PACK], BF16, name="woven%d" % h, align_bytes=64) for h in range(2)]
+        d_codes = [keep.tile([P, HALF], U32, name="d_codes%d" % h, align_bytes=64) for h in range(2)]
+        d_scale = [keep.tile([P, HALF], U8, name="d_scale%d" % h, align_bytes=64) for h in range(2)]
+        w_codes = keep.tile([P, 2 * N], U8, name="w_codes", align_bytes=64)
+        wp_codes = keep.tile([P, 2 * N], U8, name="wp_codes", align_bytes=64)
+        px_codes = keep.tile([P, 4 * J], U8, name="px_codes", align_bytes=64)
+        w_scale = keep.tile([P, N], U8, name="w_scale", align_bytes=64)
+        wp_scale = keep.tile([P, N], U8, name="wp_scale", align_bytes=64)
+        px_scale = keep.tile([P, J], U8, name="px_scale", align_bytes=64)
+        warm = keep.tile([P, 8], F32, name="warm")
+
+        rows = xf.rearrange("(p t) c -> p t c", t=PACK)
+        nc.sync.dma_start(offsets[:], offs)
+        for t in range(PACK):
+            nc.sync.dma_start(out=planes[t][:], in_=rows[:, t, :])
+        nc.sync.dma_start(out=wp_codes[:].bitcast(I32), in_=wp_words[0].bitcast(I32))
+        nc.sync.dma_start(out=px_codes[:].bitcast(I32), in_=px_words[0].rearrange("p n t -> p (n t)").bitcast(I32))
+        nc.sync.dma_start(out=w_codes[:].bitcast(I32), in_=w_words[0].bitcast(I32))
+
+        for plane, source, queue in ((wp_scale, wp_scales, nc.gpsimd), (px_scale, px_scales, nc.gpsimd), (w_scale, w_scales, nc.sync)):
+            nc.vector.memset(plane[:].bitcast(I32), 0)
+            for q in range(4):
+                queue.dma_start(out=plane[32 * q : 32 * q + 4, :].bitcast(I32), in_=source[0, 4 * q : 4 * q + 4, :].bitcast(I32))
+        for t in range(PACK):
+            nc.vector.memset(picked[t][:, 0:LEAD], 0.0)
+        nc.scalar.activation(warm[:], picked[0][:, 0:LEAD], SIGMOID)
+
+        def gather(t, j0, j1):
+            nc.vector.tensor_copy(picked[t][:, LEAD + j0 : LEAD + j1], planes[t][:].indirect(offsets[:, j0 // 16 : j1 // 16]))
+
+        def subtract(t, j0, j1):
+            nc.vector.tensor_tensor(steps[:, t, j0:j1], picked[t][:, LEAD + j0 : LEAD + j1], picked[t][:, LEAD - 1 + j0 : LEAD - 1 + j1], SUB)
+
+        def pair(h, t0):
+            return woven[h][:, :, t0 : t0 + 2], steps[:, t0 : t0 + 2, h * HALF : (h + 1) * HALF].rearrange("p t j -> p j t")
+
+        def multiply(name, h, m, weights, weight_scale, moving, moving_scale):
+            bank = psum.tile([P, 2, HALF], F32, name="%s%d%d" % (name, h, m))
+            for a in range(2):
+                n0 = (2 * m + a) * P
+                nc.tensor.matmul_mx(
+                    out=bank[:, a, :],
+                    lhsT=weights[:, 2 * n0 : 2 * (n0 + P)].bitcast(FP4X4),
+                    lhsT_scale=weight_scale[:, n0 : n0 + P],
+                    rhs=moving,
+                    rhs_scale=moving_scale,
+                    start=True,
+                    stop=True,
+                )
+            return bank
+
+        for t in range(PACK - 1):
+            gather(t, 0, J)
+            subtract(t, 0, J)
+            if t == 1:
+                for h in range(2):
+                    nc.scalar.copy(*pair(h, 0))
+
+        gates = {}
+        for h in range(2):
+            for m in range(2):
+                bank = multiply("q", h, m, wp_codes, wp_scale, px_codes[:, 4 * h * HALF : 4 * (h + 1) * HALF].bitcast(FP8X4), px_scale[:, h * HALF : (h + 1) * HALF])
+                gate = keep.tile([P, 2, HALF], F32, name="gate%d%d" % (h, m))
+                nc.scalar.activation(gate[:], bank[:], SIGMOID)
+                gates[h, m] = gate
+
+        for h in range(2):
+            gather(PACK - 1, h * HALF, (h + 1) * HALF)
+        for h in range(2):
+            subtract(PACK - 1, h * HALF, (h + 1) * HALF)
+        for h in range(2):
+            nc.vector.tensor_copy(*pair(h, 2))
+        for h in range(2):
+            nc.vector.quantize_mx(out=d_codes[h][:].bitcast(FP8X4), scales=d_scale[h][:], in_=woven[h][:].rearrange("p j t -> p (j t)"))
+        for h in range(2):
+            for m in range(2):
+                bank = multiply("p", h, m, w_codes, w_scale, d_codes[h][:].bitcast(FP8X4), d_scale[h][:])
+                result = keep.tile([P, 2, HALF], F32, name="result%d%d" % (h, m))
+                nc.vector.tensor_tensor(result[:], bank[:], gates[h, m][:], MULT)
+                nc.sync.dma_start(
+                    out=out[2 * m * P : 2 * (m + 1) * P, h * HALF : (h + 1) * HALF].rearrange("(a p) j -> p a j", p=P),
+                    in_=result[:],
+                )

@@ -45,14 +45,15 @@ def tile_list_steps_along_track_kernel(tc, xf, w_words, w_scales, px_words, px_s
         warm = keep.tile([P, 8], F32, name="warm")
 
         rows = xf.rearrange("(p t) c -> p t c", t=PACK)
-        nc.sync.dma_start(offsets[:], offs)
         for t in range(PACK):
             nc.sync.dma_start(out=planes[t][:], in_=rows[:, t, :])
+            if t == 0:
+                nc.sync.dma_start(offsets[:], offs)
         nc.sync.dma_start(out=wp_codes[:].bitcast(I32), in_=wp_words[0].bitcast(I32))
         nc.sync.dma_start(out=px_codes[:].bitcast(I32), in_=px_words[0].rearrange("p n t -> p (n t)").bitcast(I32))
         nc.sync.dma_start(out=w_codes[:].bitcast(I32), in_=w_words[0].bitcast(I32))
 
-        for plane, source, queue in ((wp_scale, wp_scales, nc.gpsimd), (px_scale, px_scales, nc.gpsimd), (w_scale, w_scales, nc.sync)):
+        for plane, source, queue in ((wp_scale, wp_scales, nc.gpsimd), (px_scale, px_scales, nc.scalar), (w_scale, w_scales, nc.gpsimd)):
             nc.vector.memset(plane[:].bitcast(I32), 0)
             for q in range(4):
                 queue.dma_start(out=plane[32 * q : 32 * q + 4, :].bitcast(I32), in_=source[0, 4 * q : 4 * q + 4, :].bitcast(I32))
@@ -110,9 +111,11 @@ def tile_list_steps_along_track_kernel(tc, xf, w_words, w_scales, px_words, px_s
         for h in range(2):
             for m in range(2):
                 bank = multiply("p", h, m, w_codes, w_scale, d_codes[h][:].bitcast(FP8X4), d_scale[h][:])
-                result = keep.tile([P, 2, HALF], F32, name="result%d%d" % (h, m))
-                nc.vector.tensor_tensor(result[:], bank[:], gates[h, m][:], MULT)
-                nc.sync.dma_start(
-                    out=out[2 * m * P : 2 * (m + 1) * P, h * HALF : (h + 1) * HALF].rearrange("(a p) j -> p a j", p=P),
-                    in_=result[:],
-                )
+                pieces = ((0, 1), (1, 2)) if (h, m) == (1, 1) else ((0, 2),)
+                for a0, a1 in pieces:
+                    result = keep.tile([P, a1 - a0, HALF], F32, name="result%d%d%d" % (h, m, a0))
+                    nc.vector.tensor_tensor(result[:], bank[:, a0:a1, :], gates[h, m][:, a0:a1, :], MULT)
+                    nc.sync.dma_start(
+                        out=out[(2 * m + a0) * P : (2 * m + a1) * P, h * HALF : (h + 1) * HALF].rearrange("(a p) j -> p a j", p=P),
+                        in_=result[:],
+                    )

@@ -45,18 +45,30 @@ def tile_list_steps_along_track_kernel(tc, xf, w_words, w_scales, px_words, px_s
         warm = keep.tile([P, 8], F32, name="warm")
 
         rows = xf.rearrange("(p t) c -> p t c", t=PACK)
-        for t in range(PACK):
+        for plane in (wp_scale, px_scale, w_scale):
+            nc.vector.memset(plane[:].bitcast(I32), 0)
+
+        def load_plane(t):
             nc.sync.dma_start(out=planes[t][:], in_=rows[:, t, :])
-            if t == 0:
-                nc.sync.dma_start(offsets[:], offs)
+
+        scale_rows = [(plane, source, q) for plane, source in ((wp_scale, wp_scales), (px_scale, px_scales), (w_scale, w_scales)) for q in range(4)]
+
+        def load_scales(i0, i1):
+            for plane, source, q in scale_rows[i0:i1]:
+                nc.sync.dma_start(out=plane[32 * q : 32 * q + 4, :].bitcast(I32), in_=source[0, 4 * q : 4 * q + 4, :].bitcast(I32))
+
+        load_plane(0)
+        nc.sync.dma_start(offsets[:], offs)
+        load_plane(1)
+        load_scales(0, 5)
+        load_plane(2)
+        load_scales(5, 6)
+        load_plane(3)
+        load_scales(6, 8)
         nc.sync.dma_start(out=wp_codes[:].bitcast(I32), in_=wp_words[0].bitcast(I32))
         nc.sync.dma_start(out=px_codes[:].bitcast(I32), in_=px_words[0].rearrange("p n t -> p (n t)").bitcast(I32))
         nc.sync.dma_start(out=w_codes[:].bitcast(I32), in_=w_words[0].bitcast(I32))
-
-        for plane, source, queue in ((wp_scale, wp_scales, nc.gpsimd), (px_scale, px_scales, nc.scalar), (w_scale, w_scales, nc.gpsimd)):
-            nc.vector.memset(plane[:].bitcast(I32), 0)
-            for q in range(4):
-                queue.dma_start(out=plane[32 * q : 32 * q + 4, :].bitcast(I32), in_=source[0, 4 * q : 4 * q + 4, :].bitcast(I32))
+        load_scales(8, 12)
         for t in range(PACK):
             nc.vector.memset(picked[t][:, 0:LEAD], 0.0)
         nc.scalar.activation(warm[:], picked[0][:, 0:LEAD], SIGMOID)
@@ -70,10 +82,10 @@ def tile_list_steps_along_track_kernel(tc, xf, w_words, w_scales, px_words, px_s
         def pair(h, t0):
             return woven[h][:, :, t0 : t0 + 2], steps[:, t0 : t0 + 2, h * HALF : (h + 1) * HALF].rearrange("p t j -> p j t")
 
-        def multiply(name, h, m, weights, weight_scale, moving, moving_scale):
-            bank = psum.tile([P, 2, HALF], F32, name="%s%d%d" % (name, h, m))
-            for a in range(2):
-                n0 = (2 * m + a) * P
+        def multiply(tag, n_tiles, weights, weight_scale, moving, moving_scale):
+            bank = psum.tile([P, len(n_tiles), HALF], F32, name=tag, tag=tag)
+            for a, n_tile in enumerate(n_tiles):
+                n0 = n_tile * P
                 nc.tensor.matmul_mx(
                     out=bank[:, a, :],
                     lhsT=weights[:, 2 * n0 : 2 * (n0 + P)].bitcast(FP4X4),
@@ -92,30 +104,37 @@ def tile_list_steps_along_track_kernel(tc, xf, w_words, w_scales, px_words, px_s
                 for h in range(2):
                     nc.scalar.copy(*pair(h, 0))
 
-        gates = {}
-        for h in range(2):
-            for m in range(2):
-                bank = multiply("q", h, m, wp_codes, wp_scale, px_codes[:, 4 * h * HALF : 4 * (h + 1) * HALF].bitcast(FP8X4), px_scale[:, h * HALF : (h + 1) * HALF])
-                gate = keep.tile([P, 2, HALF], F32, name="gate%d%d" % (h, m))
-                nc.scalar.activation(gate[:], bank[:], SIGMOID)
-                gates[h, m] = gate
+        gates = [keep.tile([P, 4, HALF], F32, name="gate%d" % h) for h in range(2)]
 
+        def make_gates(h):
+            for m in range(2):
+                bank = multiply("q%d%d" % (h, m), (2 * m, 2 * m + 1), wp_codes, wp_scale, px_codes[:, 4 * h * HALF : 4 * (h + 1) * HALF].bitcast(FP8X4), px_scale[:, h * HALF : (h + 1) * HALF])
+                nc.scalar.activation(gates[h][:, 2 * m : 2 * m + 2, :], bank[:], SIGMOID)
+
+        def products(h, groups):
+            return [multiply(tag, n_tiles, w_codes, w_scale, d_codes[h][:].bitcast(FP8X4), d_scale[h][:]) for tag, n_tiles in groups]
+
+        def finish(h, bank, n_tiles, a0, a1):
+            first, last = n_tiles[a0], n_tiles[a1 - 1] + 1
+            result = keep.tile([P, a1 - a0, HALF], F32, name="result%d%d" % (h, first))
+            nc.vector.tensor_tensor(result[:], bank[:, a0:a1, :], gates[h][:, first:last, :], MULT)
+            nc.sync.dma_start(out=out[first * P : last * P, h * HALF : (h + 1) * HALF].rearrange("(a p) j -> p a j", p=P), in_=result[:])
+
+        make_gates(0)
         for h in range(2):
             gather(PACK - 1, h * HALF, (h + 1) * HALF)
         for h in range(2):
             subtract(PACK - 1, h * HALF, (h + 1) * HALF)
         for h in range(2):
             nc.vector.tensor_copy(*pair(h, 2))
-        for h in range(2):
             nc.vector.quantize_mx(out=d_codes[h][:].bitcast(FP8X4), scales=d_scale[h][:], in_=woven[h][:].rearrange("p j t -> p (j t)"))
-        for h in range(2):
-            for m in range(2):
-                bank = multiply("p", h, m, w_codes, w_scale, d_codes[h][:].bitcast(FP8X4), d_scale[h][:])
-                pieces = ((0, 1), (1, 2)) if (h, m) == (1, 1) else ((0, 2),)
-                for a0, a1 in pieces:
-                    result = keep.tile([P, a1 - a0, HALF], F32, name="result%d%d%d" % (h, m, a0))
-                    nc.vector.tensor_tensor(result[:], bank[:, a0:a1, :], gates[h, m][:, a0:a1, :], MULT)
-                    nc.sync.dma_start(
-                        out=out[(2 * m + a0) * P : (2 * m + a1) * P, h * HALF : (h + 1) * HALF].rearrange("(a p) j -> p a j", p=P),
-                        in_=result[:],
-                    )
+        groups = (("p00", (0,)), ("p01", (1,)), ("p02", (2, 3)))
+        banks = products(0, groups)
+        make_gates(1)
+        for bank, (tag, n_tiles) in zip(banks, groups):
+            finish(0, bank, n_tiles, 0, len(n_tiles))
+        groups = (("p10", (0, 1)), ("q00", (2, 3)))
+        banks = products(1, groups)
+        finish(1, banks[0], groups[0][1], 0, 2)
+        finish(1, banks[1], groups[1][1], 0, 1)
+        finish(1, banks[1], groups[1][1], 1, 2)

@@ -38,7 +38,7 @@ def tile_list_steps_along_track_kernel(tc, xf, w_words, w_scales, px_words, px_s
         d_scale = [keep.tile([P, HALF], U8, name="d_scale%d" % h, align_bytes=64) for h in range(2)]
         w_codes = keep.tile([P, 2 * N], U8, name="w_codes", align_bytes=64)
         wp_codes = keep.tile([P, 2 * N], U8, name="wp_codes", align_bytes=64)
-        px_codes = keep.tile([P, 4 * J], U8, name="px_codes", align_bytes=64)
+        px_codes = [keep.tile([P, 4 * HALF], U8, name="px_codes%d" % h, align_bytes=64) for h in range(2)]
         w_scale = keep.tile([P, N], U8, name="w_scale", align_bytes=64)
         wp_scale = keep.tile([P, N], U8, name="wp_scale", align_bytes=64)
         px_scale = keep.tile([P, J], U8, name="px_scale", align_bytes=64)
@@ -59,16 +59,18 @@ def tile_list_steps_along_track_kernel(tc, xf, w_words, w_scales, px_words, px_s
 
         load_plane(0)
         nc.sync.dma_start(offsets[:], offs)
+        load_scales(0, 3)
         load_plane(1)
-        load_scales(0, 5)
+        load_scales(3, 5)
         load_plane(2)
-        load_scales(5, 6)
+        load_scales(5, 9)
         load_plane(3)
-        load_scales(6, 8)
         nc.sync.dma_start(out=wp_codes[:].bitcast(I32), in_=wp_words[0].bitcast(I32))
-        nc.sync.dma_start(out=px_codes[:].bitcast(I32), in_=px_words[0].rearrange("p n t -> p (n t)").bitcast(I32))
+        px_rows = px_words[0].rearrange("p n t -> p (n t)").bitcast(I32)
+        for h in range(2):
+            nc.sync.dma_start(out=px_codes[h][:].bitcast(I32), in_=px_rows[:, h * HALF : (h + 1) * HALF])
         nc.sync.dma_start(out=w_codes[:].bitcast(I32), in_=w_words[0].bitcast(I32))
-        load_scales(8, 12)
+        load_scales(9, 12)
         for t in range(PACK):
             nc.vector.memset(picked[t][:, 0:LEAD], 0.0)
         nc.scalar.activation(warm[:], picked[0][:, 0:LEAD], SIGMOID)
@@ -108,7 +110,7 @@ def tile_list_steps_along_track_kernel(tc, xf, w_words, w_scales, px_words, px_s
 
         def make_gates(h):
             for m in range(2):
-                bank = multiply("q%d%d" % (h, m), (2 * m, 2 * m + 1), wp_codes, wp_scale, px_codes[:, 4 * h * HALF : 4 * (h + 1) * HALF].bitcast(FP8X4), px_scale[:, h * HALF : (h + 1) * HALF])
+                bank = multiply("q%d%d" % (h, m), (2 * m, 2 * m + 1), wp_codes, wp_scale, px_codes[h][:].bitcast(FP8X4), px_scale[:, h * HALF : (h + 1) * HALF])
                 nc.scalar.activation(gates[h][:, 2 * m : 2 * m + 2, :], bank[:], SIGMOID)
 
         def products(h, groups):

from contextlib import ExitStack

import concourse.mybir as mybir

K, T, J, N = 512, 2048, 512, 512
FLOPS = 2 * 2 * K * N * J

F32 = mybir.dt.float32
BF16 = mybir.dt.bfloat16
I32 = mybir.dt.int32
U32 = mybir.dt.uint32
U16 = mybir.dt.uint16
U8 = mybir.dt.uint8
FP8X4 = mybir.dt.float8_e4m3fn_x4
FP4X4 = mybir.dt.float4_e2m1fn_x4
SUB = mybir.AluOpType.subtract
MULT = mybir.AluOpType.mult
SIGMOID = mybir.ActivationFunctionType.Sigmoid

P = 128
PACK = 4
HALF = J // 2
LEAD = 8


def tile_list_steps_along_track_kernel(tc, xf, w_words, w_scales, px_words, px_scales, wp_words, wp_scales, offs, out):
    nc = tc.nc
    with ExitStack() as ctx:
        keep = ctx.enter_context(tc.tile_pool(name="keep", bufs=1))
        psum = ctx.enter_context(tc.psum_pool(name="psum", bufs=1))

        offsets = keep.tile([P, J // 16], U16, name="offsets")
        planes = [keep.tile([P, T], F32, name="plane%d" % t) for t in range(PACK)]
        picked = [keep.tile([P, LEAD + J], F32, name="picked%d" % t) for t in range(PACK)]
        steps = keep.tile([P, PACK, J], BF16, name="steps")
        woven = [keep.tile([P, HALF, PACK], BF16, name="woven%d" % h, align_bytes=64) for h in range(2)]
        d_codes = [keep.tile([P, HALF], U32, name="d_codes%d" % h, align_bytes=64) for h in range(2)]
        d_scale = [keep.tile([P, HALF], U8, name="d_scale%d" % h, align_bytes=64) for h in range(2)]
        w_codes = keep.tile([P, 2 * N], U8, name="w_codes", align_bytes=64)
        wp_codes = keep.tile([P, 2 * N], U8, name="wp_codes", align_bytes=64)
        px_codes = [keep.tile([P, 4 * HALF], U8, name="px_codes%d" % h, align_bytes=64) for h in range(2)]
        w_scale = keep.tile([P, N], U8, name="w_scale", align_bytes=64)
        wp_scale = keep.tile([P, N], U8, name="wp_scale", align_bytes=64)
        px_scale = keep.tile([P, J], U8, name="px_scale", align_bytes=64)
        warm = keep.tile([P, 8], F32, name="warm")

        rows = xf.rearrange("(p t) c -> p t c", t=PACK)
        for plane in (wp_scale, px_scale, w_scale):
            nc.vector.memset(plane[:].bitcast(I32), 0)

        def load_plane(t):
            nc.sync.dma_start(out=planes[t][:], in_=rows[:, t, :])

        scale_rows = [(plane, source, q) for plane, source in ((wp_scale, wp_scales), (px_scale, px_scales), (w_scale, w_scales)) for q in range(4)]

        def load_scales(i0, i1):
            for plane, source, q in scale_rows[i0:i1]:
                nc.sync.dma_start(out=plane[32 * q : 32 * q + 4, :].bitcast(I32), in_=source[0, 4 * q : 4 * q + 4, :].bitcast(I32))

        load_plane(0)
        nc.sync.dma_start(offsets[:], offs)
        load_scales(0, 3)
        load_plane(1)
        load_scales(3, 5)
        load_plane(2)
        load_scales(5, 9)
        load_plane(3)
        nc.sync.dma_start(out=wp_codes[:].bitcast(I32), in_=wp_words[0].bitcast(I32))
        px_rows = px_words[0].rearrange("p n t -> p (n t)").bitcast(I32)
        for h in range(2):
            nc.sync.dma_start(out=px_codes[h][:].bitcast(I32), in_=px_rows[:, h * HALF : (h + 1) * HALF])
        nc.sync.dma_start(out=w_codes[:].bitcast(I32), in_=w_words[0].bitcast(I32))
        load_scales(9, 12)
        for t in range(PACK):
            nc.vector.memset(picked[t][:, 0:LEAD], 0.0)
        nc.scalar.activation(warm[:], picked[0][:, 0:LEAD], SIGMOID)

        def gather(t, j0, j1):
            nc.vector.tensor_copy(picked[t][:, LEAD + j0 : LEAD + j1], planes[t][:].indirect(offsets[:, j0 // 16 : j1 // 16]))

        def subtract(t, j0, j1):
            nc.vector.tensor_tensor(steps[:, t, j0:j1], picked[t][:, LEAD + j0 : LEAD + j1], picked[t][:, LEAD - 1 + j0 : LEAD - 1 + j1], SUB)

        def pair(h, t0):
            return woven[h][:, :, t0 : t0 + 2], steps[:, t0 : t0 + 2, h * HALF : (h + 1) * HALF].rearrange("p t j -> p j t")

        def multiply(tag, n_tiles, weights, weight_scale, moving, moving_scale):
            bank = psum.tile([P, len(n_tiles), HALF], F32, name=tag, tag=tag)
            for a, n_tile in enumerate(n_tiles):
                n0 = n_tile * P
                nc.tensor.matmul_mx(
                    out=bank[:, a, :],
                    lhsT=weights[:, 2 * n0 : 2 * (n0 + P)].bitcast(FP4X4),
                    lhsT_scale=weight_scale[:, n0 : n0 + P],
                    rhs=moving,
                    rhs_scale=moving_scale,
                    start=True,
                    stop=True,
                )
            return bank

        for t in range(PACK - 1):
            gather(t, 0, J)
            subtract(t, 0, J)
            if t == 1:
                for h in range(2):
                    nc.scalar.copy(*pair(h, 0))

        gates = [keep.tile([P, 4, HALF], F32, name="gate%d" % h) for h in range(2)]

        def make_gates(h):
            for m in range(2):
                bank = multiply("q%d%d" % (h, m), (2 * m, 2 * m + 1), wp_codes, wp_scale, px_codes[h][:].bitcast(FP8X4), px_scale[:, h * HALF : (h + 1) * HALF])
                nc.scalar.activation(gates[h][:, 2 * m : 2 * m + 2, :], bank[:], SIGMOID)

        def products(h, groups):
            return [multiply(tag, n_tiles, w_codes, w_scale, d_codes[h][:].bitcast(FP8X4), d_scale[h][:]) for tag, n_tiles in groups]

        def finish(h, bank, n_tiles, a0, a1):
            first, last = n_tiles[a0], n_tiles[a1 - 1] + 1
            result = keep.tile([P, a1 - a0, HALF], F32, name="result%d%d" % (h, first))
            nc.vector.tensor_tensor(result[:], bank[:, a0:a1, :], gates[h][:, first:last, :], MULT)
            nc.sync.dma_start(out=out[first * P : last * P, h * HALF : (h + 1) * HALF].rearrange("(a p) j -> p a j", p=P), in_=result[:])

        make_gates(0)
        for h in range(2):
            gather(PACK - 1, h * HALF, (h + 1) * HALF)
        for h in range(2):
            subtract(PACK - 1, h * HALF, (h + 1) * HALF)
        for h in range(2):
            nc.vector.tensor_copy(*pair(h, 2))
            nc.vector.quantize_mx(out=d_codes[h][:].bitcast(FP8X4), scales=d_scale[h][:], in_=woven[h][:].rearrange("p j t -> p (j t)"))
        groups = (("p00", (0,)), ("p01", (1,)), ("p02", (2, 3)))
        banks = products(0, groups)
        make_gates(1)
        for bank, (tag, n_tiles) in zip(banks, groups):
            finish(0, bank, n_tiles, 0, len(n_tiles))
        groups = (("p10", (0, 1)), ("q00", (2, 3)))
        banks = products(1, groups)
        finish(1, banks[0], groups[0][1], 0, 2)
        finish(1, banks[1], groups[1][1], 0, 1)
        finish(1, banks[1], groups[1][1], 1, 2)
